import numpy as np
import ml_dtypes


def mxq(x, axis, fmt="e4m3"):
    dtype, down = {"e4m3": (ml_dtypes.float8_e4m3fn, 7), "e5m2": (ml_dtypes.float8_e5m2, 14)}[fmt]
    v = np.moveaxis(np.asarray(x, np.float32).astype(ml_dtypes.bfloat16).astype(np.float64), axis, -1)
    blocks = v.reshape(v.shape[:-1] + (-1, 32))
    amax = np.abs(blocks).max(-1, keepdims=True)
    byte = np.maximum(np.where(amax > 0, np.frexp(amax)[1] - 1 + 127, 0) - down, 1)
    scale = np.exp2(byte - 127.0)
    codes = (blocks / scale).astype(np.float32).astype(dtype).astype(np.float64)
    return np.moveaxis((codes * scale).reshape(v.shape), -1, axis)


WIDE = False


def mx_kscale(k):
    if not WIDE:
        return np.ones(k)
    levels = np.array([30, -30])
    if k % 512:
        return np.exp2(np.random.permutation(np.resize(levels, k // 32))).repeat(32)
    a = np.empty((k // 512, 16))
    for p in range(k // 512):
        a[p, :8] = np.random.permutation(np.resize(levels, 8))
        for g in range(8):
            far = levels[np.abs(levels - a[p, g]) >= 10]
            a[p, g + 8] = far[np.random.randint(len(far))]
    return np.exp2(a.ravel()).repeat(32)


def f64(x):
    return np.asarray(x).astype(np.float64)


def striped(idx):
    return np.tile(np.asarray(idx).reshape(-1, 16).T, (8, 1)).astype(np.uint16)


def unstriped(offs):
    return offs[:16].T.reshape(-1).astype(np.int64)


def striped8(idx):
    return np.asarray(idx).reshape(8, -1, 16).transpose(0, 2, 1).reshape(128, -1).astype(np.uint16)


def unstriped8(offs):
    return offs.reshape(8, 16, -1).transpose(0, 2, 1).reshape(8, -1).astype(np.int64)


def pick8(x, idx, run):
    r = np.arange(len(x))
    return x[r[:, None], idx[r % (8 * run) // run]]


E2M1 = np.array([0.0, 0.5, 1.0, 1.5, 2.0, 3.0, 4.0, 6.0, -0.0, -0.5, -1.0, -1.5, -2.0, -3.0, -4.0, -6.0])


def pack_weight(w, fmt):
    k, n = w.shape
    w = f64(np.asarray(w, np.float32).astype(ml_dtypes.bfloat16)).reshape(k // 32, 32, n)
    amax = np.abs(w).max(1)
    if fmt in ("e4m3", "e5m2"):
        byte = np.frexp(amax)[1] - 1 + 127 - (7 if fmt == "e4m3" else 14)
    else:
        mant, ex = np.frexp(amax / 6.0)
        byte = np.where(mant > 0.5, ex, ex - 1) + 127
    byte = np.clip(np.where(amax > 0, byte, 1), 1, 254)
    scaled = (w * np.exp2(127.0 - byte)[:, None, :]).reshape(k, n).astype(np.float32)
    by_word = np.ascontiguousarray(scaled.reshape(k // 512, 128, 4, n).transpose(0, 1, 3, 2))
    if fmt in ("e4m3", "e5m2"):
        words = by_word.astype(ml_dtypes.float8_e4m3fn if fmt == "e4m3" else ml_dtypes.float8_e5m2).view(np.uint8)
    else:
        c = by_word.astype(ml_dtypes.float4_e2m1fn).view(np.uint8) & 0xF
        words = (c[..., 0::2] | (c[..., 1::2] << 4)).reshape(k // 512, 128, 2 * n)
    return np.ascontiguousarray(words), np.ascontiguousarray(byte.astype(np.uint8).reshape(k // 512, 16, n))


def unpack_weight(words, scales, fmt):
    g, _, n = scales.shape
    words = np.ascontiguousarray(words).reshape(g, 128, n, -1)
    if fmt in ("e4m3", "e5m2"):
        vals = words.view(ml_dtypes.float8_e4m3fn if fmt == "e4m3" else ml_dtypes.float8_e5m2).astype(np.float64)
    else:
        nib = np.empty((g, 128, n, 4), np.uint8)
        nib[..., 0::2] = words & 0xF
        nib[..., 1::2] = words >> 4
        vals = E2M1[nib]
    vals = vals * np.repeat(np.exp2(scales.astype(np.float64) - 127.0), 8, axis=1)[..., None]
    return vals.transpose(0, 1, 3, 2).reshape(g * 512, n)


K, T, J, R, F, Z, C, D, I, O, N = 512, 1024, 256, 512, 512, 1024, 512, 512, 256, 256, 256


def setup_inputs():
    n = np.random.standard_normal
    idx = np.random.permutation(T)[:J]
    idx2 = np.random.permutation(Z)[:J]
    idx3 = np.stack([np.random.permutation(C)[:J] for _ in range(8)])
    idx4 = np.random.permutation(C)[:I]
    idx5 = np.stack([np.random.permutation(D)[:I] for _ in range(8)])
    idx6 = np.random.permutation(D)[:O]
    fk = mx_kscale(K)
    ff = mx_kscale(F)
    fr = mx_kscale(R)
    xtp = pack_weight(n((K, T)) / fk[:, None], "e5m2")
    xop = pack_weight(n((F, Z)) / ff[:, None], "e4m3")
    wp = pack_weight(n((K, R)) * 1 / np.sqrt(K) * fk[:, None] * fr, "e2m1")
    w0p = pack_weight(n((F, R)) * 1 / np.sqrt(F) * ff[:, None] * fr, "e2m1")
    wbp = pack_weight(n((R, N)) * 1 / np.sqrt(R) / fr[:, None], "e2m1")
    return {
        "xt_words": xtp[0],
        "xt_scales": xtp[1],
        "xo_words": xop[0],
        "xo_scales": xop[1],
        "w_words": wp[0],
        "w_scales": wp[1],
        "w0_words": w0p[0],
        "w0_scales": w0p[1],
        "wb_words": wbp[0],
        "wb_scales": wbp[1],
        "offs": striped(idx),
        "offs2": striped(idx2),
        "offs3": striped8(idx3),
        "offs4": striped(idx4),
        "offs5": striped8(idx5),
        "offs6": striped(idx6),
    }


def reference(xt_words, xt_scales, xo_words, xo_scales, w_words, w_scales, w0_words, w0_scales, wb_words, wb_scales, offs, offs2, offs3, offs4, offs5, offs6):
    idx = unstriped(offs)
    idx2 = unstriped(offs2)
    idx3 = unstriped8(offs3)
    idx4 = unstriped(offs4)
    idx5 = unstriped8(offs5)
    idx6 = unstriped(offs6)
    xtu = unpack_weight(xt_words, xt_scales, "e5m2")
    xou = unpack_weight(xo_words, xo_scales, "e4m3")
    wu = unpack_weight(w_words, w_scales, "e2m1")
    w0u = unpack_weight(w0_words, w0_scales, "e2m1")
    wbu = unpack_weight(wb_words, wb_scales, "e2m1")
    xtidxg = xtu[:, idx]
    xoidx2g = xou[:, idx2]
    a = wu.T @ xtidxg + w0u.T @ xoidx2g
    pa = np.zeros((R, C))
    pa[np.arange(R)[:, None], idx3[np.arange(R) % 512 // 64]] = a
    h1 = pa[:, idx4]
    pb = np.zeros((R, D))
    pb[np.arange(R)[:, None], idx5[np.arange(R) % 512 // 64]] = h1
    hid = np.maximum(pb[:, idx6], 0.0)
    hidq = mxq(hid, 0, "e4m3")
    p = wbu.T @ hidq
    return p

@@ -1,0 +1,155 @@
+from contextlib import ExitStack
+
+import concourse.mybir as mybir
+
+F32 = mybir.dt.float32
+BF16 = mybir.dt.bfloat16
+I32 = mybir.dt.int32
+U32 = mybir.dt.uint32
+U16 = mybir.dt.uint16
+U8 = mybir.dt.uint8
+E4M3 = mybir.dt.float8_e4m3fn_x4
+E5M2 = mybir.dt.float8_e5m2_x4
+E2M1 = mybir.dt.float4_e2m1fn_x4
+COPY = mybir.ActivationFunctionType.Copy
+MAX = mybir.AluOpType.max
+
+P = 128
+PACK = 4
+T, J, R, C, N = 1024, 256, 512, 512, 256
+HALF = 128
+HCOLS = HALF // 16
+FLOPS = 2 * (2 * 512 * R * J + R * N * J)
+
+
+def tile_list_tworoutes_kernel(tc, xt_words, xt_scales, xo_words, xo_scales, w_words, w_scales, w0_words, w0_scales,
+                                    wb_words, wb_scales, offs, offs2, offs3, offs4, offs5, offs6, out):
+    nc = tc.nc
+    with ExitStack() as ctx:
+        pool = ctx.enter_context(tc.tile_pool(name="keep", bufs=1))
+        psum = ctx.enter_context(tc.psum_pool(name="psum", bufs=1))
+
+        def sb(shape, dtype, name, tag=None):
+            return pool.tile(shape, dtype, name=name, tag=tag or name, align_bytes=64)
+
+        lists = [sb([P, J // 16], U16, f"list{i}") for i in range(6)]
+        x_words = [sb([P, T], U32, f"x_words{i}") for i in range(2)]
+        x_scales = [sb([P, T], U8, f"x_scales{i}") for i in range(2)]
+        xs_stage = [sb([64, 2, T], U8, f"xs_stage{i}") for i in range(2)]
+        w_raw = sb([P, 2, 2 * R], U8, "w_raw")
+        ws_raw = sb([P, 2, 2, R], U8, "ws_raw")
+        wb_raw = sb([P, 2 * N], U8, "wb_raw")
+        wb_plane = sb([P, N], U8, "wb_plane")
+        board_a = [sb([P, C], F32, f"board_a{t}") for t in range(PACK)]
+
+        xs32 = [xs_stage[i][:].rearrange("p h c -> p (h c)").bitcast(I32).rearrange("p (h c) -> p h c", h=2) for i in range(2)]
+        ws32 = ws_raw[:].rearrange("p h i c -> p (h i c)").bitcast(I32).rearrange("p (h i c) -> p h i c", h=2, i=2)
+        nc.vector.memset(xs32[0], 0)
+        nc.gpsimd.memset(xs32[1], 0)
+        nc.vector.memset(ws32[0:64], 0)
+        for t in range(PACK):
+            nc.vector.memset(board_a[t][:], 0.0)
+        nc.vector.memset(wb_plane[:].bitcast(I32), 0)
+
+        def load_words(dst, src):
+            nc.sync.dma_start(out=dst.bitcast(I32), in_=src.bitcast(I32))
+
+        def load_folded(dst, src, b):
+            rows = src[0].bitcast(I32).rearrange("(h b r) c -> b r h c", h=2, b=2)
+            nc.scalar.dma_start(out=dst[32 * b : 32 * b + 4], in_=rows[b])
+
+        for i, (lst, words, scales) in enumerate(((offs, xt_words, xt_scales), (offs2, xo_words, xo_scales))):
+            nc.sync.dma_start(lists[i][:], lst)
+            load_folded(xs32[i], scales, 0)
+            load_words(x_words[i][:], words[0].rearrange("p c r -> p (c r)"))
+            load_folded(xs32[i], scales, 1)
+        for i, (words, scales) in enumerate(((w_words, w_scales), (w0_words, w0_scales))):
+            load_words(w_raw[:, i, :], words[0])
+            load_folded(ws32[:, :, i, :], scales, 0)
+            nc.sync.dma_start(lists[2 + i][:], (offs3, offs4)[i])
+            load_folded(ws32[:, :, i, :], scales, 1)
+        nc.sync.dma_start(lists[4][:], offs5)
+        nc.sync.dma_start(lists[5][:], offs6)
+        load_words(wb_raw[:], wb_words[0])
+        wb_rows = wb_scales[0].bitcast(I32).rearrange("(q r) c -> r q c", r=4)
+        for r in range(4):
+            nc.sync.dma_start(out=wb_plane[:].bitcast(I32)[r:P:32, :], in_=wb_rows[r])
+
+        for h in range(2):
+            for i in range(2):
+                nc.vector.tensor_copy(out=x_scales[i][:].bitcast(I32)[64 * h : 64 * (h + 1)], in_=xs32[i][:, h, :])
+
+        w16 = w_raw[:].rearrange("p i c -> p (i c)").bitcast(U16).rearrange("p (i m t) -> p t i m", i=2, t=PACK)
+        ws8 = ws_raw[:, 0].rearrange("p i (m t) -> p t i m", t=PACK)
+        w_dealt = sb([P, PACK, 2, 2 * P], U8, "w_dealt")
+        ws_dealt = sb([P, PACK, 2, P], U8, "ws_dealt")
+        wd16 = w_dealt[:].rearrange("p t i c -> p (t i c)").bitcast(U16).rearrange("p (t i m) -> p t i m", t=PACK, i=2)
+
+        def gather_half(h):
+            words = [sb([P, HALF], U32, f"g_words{i}_{h}", f"g_words{i}") for i in range(2)]
+            scales = [sb([P, HALF], U8, f"g_scales{i}_{h}", f"g_scales{i}") for i in range(2)]
+            for i in range(2):
+                part = lists[i][:, HCOLS * h : HCOLS * (h + 1)]
+                nc.vector.tensor_copy(out=scales[i][:], in_=x_scales[i][:].indirect(part))
+                nc.vector.tensor_copy(out=words[i][:], in_=x_words[i][:].indirect(part))
+            return words, scales
+
+        def first_stage(h, ts, words, scales):
+            acc = psum.tile([P, len(ts), HALF], F32, name=f"acc{h}_{ts[0]}")
+            for u, t in enumerate(ts):
+                for i, fmt in enumerate((E5M2, E4M3)):
+                    nc.tensor.matmul_mx(out=acc[:, u, :], lhsT=w_dealt[:, t, i, :].bitcast(E2M1), lhsT_scale=ws_dealt[:, t, i, :],
+                                        rhs=words[i][:].bitcast(fmt), rhs_scale=scales[i][:], start=(i == 0), stop=(i == 1))
+            a_sb = sb([P, len(ts), HALF], F32, f"a{h}_{ts[0]}")
+            nc.vector.tensor_copy(out=a_sb[:], in_=acc[:])
+            for u, t in enumerate(ts):
+                nc.scalar.activation(board_a[t][:].indirect(lists[2][:, HCOLS * h : HCOLS * (h + 1)]), a_sb[:, u, :], COPY)
+
+        words, scales = gather_half(0)
+        nc.vector.tensor_copy(out=ws32[64:128, 0], in_=ws32[0:64, 1])
+        for ts in (slice(0, 1), slice(1, PACK)):
+            nc.scalar.copy(out=wd16[:, ts], in_=w16[:, ts])
+            nc.vector.tensor_copy(out=ws_dealt[:, ts], in_=ws8[:, ts])
+        for ts in ((0,), (1,), (2, 3)):
+            first_stage(0, ts, words, scales)
+        words, scales = gather_half(1)
+        for ts in ((0, 1), (2, 3)):
+            first_stage(1, ts, words, scales)
+
+        board_b = [sb([P, C], F32, f"board_b{t}", tag) for t, tag in enumerate(("x_words0", "x_words1", "w_raw", "ws_raw"))]
+        for t in range(PACK):
+            h1 = sb([P, J], F32, f"h1_{t}")
+            nc.vector.tensor_copy(out=h1[:], in_=board_a[t][:].indirect(lists[3][:]))
+            nc.vector.memset(board_b[t][:], 0.0)
+            nc.scalar.activation(board_b[t][:].indirect(lists[4][:]), h1[:], COPY)
+
+        last = PACK - 1
+        hid = sb([P, J, PACK], BF16, "hid")
+        picked = sb([P, last, J], F32, "picked")
+        for t in range(last):
+            nc.vector.tensor_copy(out=picked[:, t, :], in_=board_b[t][:].indirect(lists[5][:]))
+        nc.vector.tensor_scalar(out=hid[:, :, 0:last], in0=picked[:].rearrange("p t o -> p o t"), scalar1=0.0, scalar2=None, op0=MAX)
+        tail = [sb([P, HALF], F32, f"tail{h}") for h in range(2)]
+        nc.vector.tensor_copy(out=tail[0][:], in_=board_b[last][:].indirect(lists[5][:, 0:HCOLS]))
+        nc.scalar.activation(tail[1][:], board_b[last][:].indirect(lists[5][:, HCOLS : 2 * HCOLS]), COPY)
+        for h in range(2):
+            nc.vector.tensor_scalar(out=hid[:, HALF * h : HALF * (h + 1), last], in0=tail[h][:], scalar1=0.0, scalar2=None, op0=MAX)
+
+        out_v = out.rearrange("(m p) (h o) -> h p m o", p=P, h=2)
+        for h in range(2):
+            codes = sb([P, HALF], U32, f"codes{h}")
+            plane = sb([P, HALF], U8, f"plane{h}")
+            nc.vector.quantize_mx(out=codes[:].bitcast(E4M3), scales=plane[:],
+                                  in_=hid[:, HALF * h : HALF * (h + 1), :].rearrange("p o t -> p (o t)"))
+            res = psum.tile([P, 2, HALF], F32, name=f"res{h}")
+            for m in range(2):
+                nc.tensor.matmul_mx(out=res[:, m, :], lhsT=wb_raw[:, 2 * P * m : 2 * P * (m + 1)].bitcast(E2M1),
+                                    lhsT_scale=wb_plane[:, P * m : P * (m + 1)], rhs=codes[:].bitcast(E4M3),
+                                    rhs_scale=plane[:], start=True, stop=True)
+            res_sb = sb([P, 2, HALF], F32, f"res_sb{h}")
+            if h == 0:
+                nc.scalar.copy(out=res_sb[:], in_=res[:])
+                nc.scalar.dma_start(out=out_v[h], in_=res_sb[:])
+            else:
+                nc.vector.tensor_copy(out=res_sb[:], in_=res[:])
+                nc.sync.dma_start(out=out_v[h], in_=res_sb[:])

@@ -35,52 +35,46 @@ def tile_list_tworoutes_kernel(tc, xt_words, xt_scales, xo_words, xo_scales, w_w
         lists = [sb([P, J // 16], U16, f"list{i}") for i in range(6)]
         x_words = [sb([P, T], U32, f"x_words{i}") for i in range(2)]
         x_scales = [sb([P, T], U8, f"x_scales{i}") for i in range(2)]
-        xs_stage = [sb([64, 2, T], U8, f"xs_stage{i}") for i in range(2)]
+        xs_stage = [sb([4, 4, T], U8, f"xs_stage{i}") for i in range(2)]
+        ws_stage = sb([4, 4, 2, R], U8, "ws_stage")
         w_raw = sb([P, 2, 2 * R], U8, "w_raw")
-        ws_raw = sb([P, 2, 2, R], U8, "ws_raw")
-        wb_raw = sb([P, 2 * N], U8, "wb_raw")
-        wb_plane = sb([P, N], U8, "wb_plane")
+        ws_plane = sb([P, 2, R], U8, "ws_plane")
         board_a = [sb([P, C], F32, f"board_a{t}") for t in range(PACK)]
 
-        xs32 = [xs_stage[i][:].rearrange("p h c -> p (h c)").bitcast(I32).rearrange("p (h c) -> p h c", h=2) for i in range(2)]
-        ws32 = ws_raw[:].rearrange("p h i c -> p (h i c)").bitcast(I32).rearrange("p (h i c) -> p h i c", h=2, i=2)
-        nc.vector.memset(xs32[0], 0)
-        nc.gpsimd.memset(xs32[1], 0)
-        nc.vector.memset(ws32[0:64], 0)
+        xs32 = [xs_stage[i][:].rearrange("p q c -> p (q c)").bitcast(I32).rearrange("p (q c) -> p q c", q=4) for i in range(2)]
+        ws32 = ws_stage[:].rearrange("p q i c -> p (q i c)").bitcast(I32).rearrange("p (q i c) -> p q i c", q=4, i=2)
+        wsp32 = ws_plane[:].rearrange("p i c -> p (i c)").bitcast(I32).rearrange("p (i c) -> p i c", i=2)
         for t in range(PACK):
             nc.vector.memset(board_a[t][:], 0.0)
-        nc.vector.memset(wb_plane[:].bitcast(I32), 0)
+        for i in range(2):
+            nc.vector.memset(x_scales[i][:].bitcast(I32), 0)
+        nc.vector.memset(wsp32, 0)
 
         def load_words(dst, src):
             nc.sync.dma_start(out=dst.bitcast(I32), in_=src.bitcast(I32))
 
-        def load_folded(dst, src, b):
-            rows = src[0].bitcast(I32).rearrange("(h b r) c -> b r h c", h=2, b=2)
-            nc.scalar.dma_start(out=dst[32 * b : 32 * b + 4], in_=rows[b])
+        def load_rows(dst, src):
+            nc.scalar.dma_start(out=dst, in_=src[0].bitcast(I32).rearrange("(q r) c -> r q c", r=4))
 
-        for i, (lst, words, scales) in enumerate(((offs, xt_words, xt_scales), (offs2, xo_words, xo_scales))):
-            nc.sync.dma_start(lists[i][:], lst)
-            load_folded(xs32[i], scales, 0)
-            load_words(x_words[i][:], words[0].rearrange("p c r -> p (c r)"))
-            load_folded(xs32[i], scales, 1)
-        for i, (words, scales) in enumerate(((w_words, w_scales), (w0_words, w0_scales))):
-            load_words(w_raw[:, i, :], words[0])
-            load_folded(ws32[:, :, i, :], scales, 0)
-            nc.sync.dma_start(lists[2 + i][:], (offs3, offs4)[i])
-            load_folded(ws32[:, :, i, :], scales, 1)
-        nc.sync.dma_start(lists[4][:], offs5)
-        nc.sync.dma_start(lists[5][:], offs6)
-        load_words(wb_raw[:], wb_words[0])
-        wb_rows = wb_scales[0].bitcast(I32).rearrange("(q r) c -> r q c", r=4)
-        for r in range(4):
-            nc.sync.dma_start(out=wb_plane[:].bitcast(I32)[r:P:32, :], in_=wb_rows[r])
+        load_words(w_raw[:, 0, :], w_words[0])
+        load_rows(xs32[0], xt_scales)
+        load_words(w_raw[:, 1, :], w0_words[0])
+        load_rows(xs32[1], xo_scales)
+        nc.sync.dma_start(lists[0][:], offs)
+        load_rows(ws32[:, :, 0, :], w_scales)
+        load_words(x_words[0][:], xt_words[0].rearrange("p c r -> p (c r)"))
+        load_rows(ws32[:, :, 1, :], w0_scales)
+        load_words(x_words[1][:], xo_words[0].rearrange("p c r -> p (c r)"))
+        for i, src in enumerate((offs2, offs3, offs4, offs5, offs6)):
+            nc.sync.dma_start(lists[1 + i][:], src)
 
-        for h in range(2):
+        for q in range(4):
             for i in range(2):
-                nc.vector.tensor_copy(out=x_scales[i][:].bitcast(I32)[64 * h : 64 * (h + 1)], in_=xs32[i][:, h, :])
+                nc.vector.tensor_copy(out=x_scales[i][:].bitcast(I32)[32 * q : 32 * q + 4], in_=xs32[i][:, q, :])
+            nc.vector.tensor_copy(out=wsp32[32 * q : 32 * q + 4], in_=ws32[:, q])
 
         w16 = w_raw[:].rearrange("p i c -> p (i c)").bitcast(U16).rearrange("p (i m t) -> p t i m", i=2, t=PACK)
-        ws8 = ws_raw[:, 0].rearrange("p i (m t) -> p t i m", t=PACK)
+        ws8 = ws_plane[:].rearrange("p i (m t) -> p t i m", t=PACK)
         w_dealt = sb([P, PACK, 2, 2 * P], U8, "w_dealt")
         ws_dealt = sb([P, PACK, 2, P], U8, "ws_dealt")
         wd16 = w_dealt[:].rearrange("p t i c -> p (t i c)").bitcast(U16).rearrange("p (t i m) -> p t i m", t=PACK, i=2)
@@ -101,22 +95,32 @@ def tile_list_tworoutes_kernel(tc, xt_words, xt_scales, xo_words, xo_scales, w_w
                     nc.tensor.matmul_mx(out=acc[:, u, :], lhsT=w_dealt[:, t, i, :].bitcast(E2M1), lhsT_scale=ws_dealt[:, t, i, :],
                                         rhs=words[i][:].bitcast(fmt), rhs_scale=scales[i][:], start=(i == 0), stop=(i == 1))
             a_sb = sb([P, len(ts), HALF], F32, f"a{h}_{ts[0]}")
-            nc.vector.tensor_copy(out=a_sb[:], in_=acc[:])
+            if (h, ts[0]) == (0, 0):
+                nc.scalar.activation(a_sb[:], acc[:], COPY)
+            else:
+                nc.vector.tensor_copy(out=a_sb[:], in_=acc[:])
             for u, t in enumerate(ts):
                 nc.scalar.activation(board_a[t][:].indirect(lists[2][:, HCOLS * h : HCOLS * (h + 1)]), a_sb[:, u, :], COPY)
 
+        nc.scalar.copy(out=wd16, in_=w16)
+        nc.vector.tensor_copy(out=ws_dealt[:, 0:1], in_=ws8[:, 0:1])
         words, scales = gather_half(0)
-        nc.vector.tensor_copy(out=ws32[64:128, 0], in_=ws32[0:64, 1])
-        for ts in (slice(0, 1), slice(1, PACK)):
-            nc.scalar.copy(out=wd16[:, ts], in_=w16[:, ts])
-            nc.vector.tensor_copy(out=ws_dealt[:, ts], in_=ws8[:, ts])
+        nc.vector.tensor_copy(out=ws_dealt[:, 1:PACK], in_=ws8[:, 1:PACK])
         for ts in ((0,), (1,), (2, 3)):
             first_stage(0, ts, words, scales)
         words, scales = gather_half(1)
         for ts in ((0, 1), (2, 3)):
             first_stage(1, ts, words, scales)
 
-        board_b = [sb([P, C], F32, f"board_b{t}", tag) for t, tag in enumerate(("x_words0", "x_words1", "w_raw", "ws_raw"))]
+        wb_raw = sb([P, 2 * N], U8, "wb_raw", "x_scales0")
+        wb_plane = sb([P, N], U8, "wb_plane", "x_scales1")
+        nc.vector.memset(wb_plane[:].bitcast(I32), 0)
+        load_words(wb_raw[:], wb_words[0])
+        wb_rows = wb_scales[0].bitcast(I32).rearrange("(q r) c -> r q c", r=4)
+        for r in range(4):
+            nc.sync.dma_start(out=wb_plane[:].bitcast(I32)[r:P:32, :], in_=wb_rows[r])
+
+        board_b = [sb([P, C], F32, f"board_b{t}", tag) for t, tag in enumerate(("x_words0", "x_words1", "w_raw", "ws_plane"))]
         for t in range(PACK):
             h1 = sb([P, J], F32, f"h1_{t}")
             nc.vector.tensor_copy(out=h1[:], in_=board_a[t][:].indirect(lists[3][:]))

@@ -35,19 +35,21 @@ def tile_list_tworoutes_kernel(tc, xt_words, xt_scales, xo_words, xo_scales, w_w
         lists = [sb([P, J // 16], U16, f"list{i}") for i in range(6)]
         x_words = [sb([P, T], U32, f"x_words{i}") for i in range(2)]
         x_scales = [sb([P, T], U8, f"x_scales{i}") for i in range(2)]
-        xs_stage = [sb([4, 4, T], U8, f"xs_stage{i}") for i in range(2)]
+        xs_stage = sb([4, 4, T], U8, "xs_stage")
         ws_stage = sb([4, 4, 2, R], U8, "ws_stage")
         w_raw = sb([P, 2, 2 * R], U8, "w_raw")
         ws_plane = sb([P, 2, R], U8, "ws_plane")
         board_a = [sb([P, C], F32, f"board_a{t}") for t in range(PACK)]
 
-        xs32 = [xs_stage[i][:].rearrange("p q c -> p (q c)").bitcast(I32).rearrange("p (q c) -> p q c", q=4) for i in range(2)]
+        xs32 = xs_stage[:].rearrange("p q c -> p (q c)").bitcast(I32).rearrange("p (q c) -> p q c", q=4)
         ws32 = ws_stage[:].rearrange("p q i c -> p (q i c)").bitcast(I32).rearrange("p (q i c) -> p q i c", q=4, i=2)
         wsp32 = ws_plane[:].rearrange("p i c -> p (i c)").bitcast(I32).rearrange("p (i c) -> p i c", i=2)
-        for t in range(PACK):
+        for t in range(2):
             nc.vector.memset(board_a[t][:], 0.0)
-        for i in range(2):
-            nc.vector.memset(x_scales[i][:].bitcast(I32), 0)
+        nc.vector.memset(x_scales[1][:].bitcast(I32), 0)
+        for t in range(2, PACK):
+            nc.vector.memset(board_a[t][:], 0.0)
+        nc.vector.memset(x_scales[0][:].bitcast(I32), 0)
         nc.vector.memset(wsp32, 0)
 
         def load_words(dst, src):
@@ -56,44 +58,45 @@ def tile_list_tworoutes_kernel(tc, xt_words, xt_scales, xo_words, xo_scales, w_w
         def load_rows(dst, src):
             nc.scalar.dma_start(out=dst, in_=src[0].bitcast(I32).rearrange("(q r) c -> r q c", r=4))
 
+        def load_plane(dst, src):
+            rows = src[0].bitcast(I32).rearrange("(q r) c -> r q c", r=4)
+            for r in range(4):
+                nc.sync.dma_start(out=dst[:].bitcast(I32)[r:P:32, :], in_=rows[r])
+
         load_words(w_raw[:, 0, :], w_words[0])
-        load_rows(xs32[0], xt_scales)
+        load_rows(xs32, xt_scales)
         load_words(w_raw[:, 1, :], w0_words[0])
-        load_rows(xs32[1], xo_scales)
-        nc.sync.dma_start(lists[0][:], offs)
         load_rows(ws32[:, :, 0, :], w_scales)
-        load_words(x_words[0][:], xt_words[0].rearrange("p c r -> p (c r)"))
+        nc.sync.dma_start(lists[0][:], offs)
         load_rows(ws32[:, :, 1, :], w0_scales)
+        nc.sync.dma_start(lists[1][:], offs2)
+        load_words(x_words[0][:], xt_words[0].rearrange("p c r -> p (c r)"))
+        nc.sync.dma_start(lists[2][:], offs3)
         load_words(x_words[1][:], xo_words[0].rearrange("p c r -> p (c r)"))
-        for i, src in enumerate((offs2, offs3, offs4, offs5, offs6)):
-            nc.sync.dma_start(lists[1 + i][:], src)
+        for i, src in ((3, offs4), (4, offs5), (5, offs6)):
+            nc.sync.dma_start(lists[i][:], src)
+        load_plane(x_scales[1], xo_scales)
 
         for q in range(4):
-            for i in range(2):
-                nc.vector.tensor_copy(out=x_scales[i][:].bitcast(I32)[32 * q : 32 * q + 4], in_=xs32[i][:, q, :])
+            nc.vector.tensor_copy(out=x_scales[0][:].bitcast(I32)[32 * q : 32 * q + 4], in_=xs32[:, q, :])
             nc.vector.tensor_copy(out=wsp32[32 * q : 32 * q + 4], in_=ws32[:, q])
 
         w16 = w_raw[:].rearrange("p i c -> p (i c)").bitcast(U16).rearrange("p (i m t) -> p t i m", i=2, t=PACK)
         ws8 = ws_plane[:].rearrange("p i (m t) -> p t i m", t=PACK)
         w_dealt = sb([P, PACK, 2, 2 * P], U8, "w_dealt")
-        ws_dealt = sb([P, PACK, 2, P], U8, "ws_dealt")
         wd16 = w_dealt[:].rearrange("p t i c -> p (t i c)").bitcast(U16).rearrange("p (t i m) -> p t i m", t=PACK, i=2)
 
-        def gather_half(h):
-            words = [sb([P, HALF], U32, f"g_words{i}_{h}", f"g_words{i}") for i in range(2)]
-            scales = [sb([P, HALF], U8, f"g_scales{i}_{h}", f"g_scales{i}") for i in range(2)]
-            for i in range(2):
-                part = lists[i][:, HCOLS * h : HCOLS * (h + 1)]
-                nc.vector.tensor_copy(out=scales[i][:], in_=x_scales[i][:].indirect(part))
-                nc.vector.tensor_copy(out=words[i][:], in_=x_words[i][:].indirect(part))
-            return words, scales
+        def gather(table, i, h, dtype, name):
+            got = sb([P, HALF], dtype, f"{name}_{h}", name)
+            nc.vector.tensor_copy(out=got[:], in_=table[:].indirect(lists[i][:, HCOLS * h : HCOLS * (h + 1)]))
+            return got[:]
 
         def first_stage(h, ts, words, scales):
             acc = psum.tile([P, len(ts), HALF], F32, name=f"acc{h}_{ts[0]}")
             for u, t in enumerate(ts):
                 for i, fmt in enumerate((E5M2, E4M3)):
-                    nc.tensor.matmul_mx(out=acc[:, u, :], lhsT=w_dealt[:, t, i, :].bitcast(E2M1), lhsT_scale=ws_dealt[:, t, i, :],
-                                        rhs=words[i][:].bitcast(fmt), rhs_scale=scales[i][:], start=(i == 0), stop=(i == 1))
+                    nc.tensor.matmul_mx(out=acc[:, u, :], lhsT=w_dealt[:, t, i, :].bitcast(E2M1), lhsT_scale=ws_dealt[t][:, i, :],
+                                        rhs=words[i].bitcast(fmt), rhs_scale=scales[i], start=(i == 0), stop=(i == 1))
             a_sb = sb([P, len(ts), HALF], F32, f"a{h}_{ts[0]}")
             if (h, ts[0]) == (0, 0):
                 nc.scalar.activation(a_sb[:], acc[:], COPY)
@@ -103,24 +106,30 @@ def tile_list_tworoutes_kernel(tc, xt_words, xt_scales, xo_words, xo_scales, w_w
                 nc.scalar.activation(board_a[t][:].indirect(lists[2][:, HCOLS * h : HCOLS * (h + 1)]), a_sb[:, u, :], COPY)
 
         nc.scalar.copy(out=wd16, in_=w16)
-        nc.vector.tensor_copy(out=ws_dealt[:, 0:1], in_=ws8[:, 0:1])
-        words, scales = gather_half(0)
-        nc.vector.tensor_copy(out=ws_dealt[:, 1:PACK], in_=ws8[:, 1:PACK])
+        ws_first = sb([P, 2, P], U8, "ws_first")
+        nc.vector.tensor_copy(out=ws_first[:], in_=ws8[:, 0])
+        xt_s = gather(x_scales[0], 0, 0, U8, "g_xt_scales")
+        words = [gather(x_words[i], i, 0, U32, f"g_words{i}") for i in range(2)]
+        xo_s = sb([P, J], U8, "g_xo_scales")
+        nc.vector.tensor_copy(out=xo_s[:], in_=x_scales[1][:].indirect(lists[1][:]))
+        ws_rest = sb([P, PACK - 1, 2, P], U8, "ws_rest", "x_scales1")
+        nc.vector.tensor_copy(out=ws_rest[:, 0:1], in_=ws8[:, 1:2])
+        nc.vector.tensor_copy(out=ws_rest[:, 1:3], in_=ws8[:, 2:PACK])
+        ws_dealt = [ws_first[:]] + [ws_rest[:, u] for u in range(PACK - 1)]
         for ts in ((0,), (1,), (2, 3)):
-            first_stage(0, ts, words, scales)
-        words, scales = gather_half(1)
-        for ts in ((0, 1), (2, 3)):
-            first_stage(1, ts, words, scales)
+            first_stage(0, ts, words, [xt_s, xo_s[:, 0:HALF]])
+        xt_s = gather(x_scales[0], 0, 1, U8, "g_xt_scales")
+        words = [gather(x_words[i], i, 1, U32, f"g_words{i}") for i in range(2)]
+        for ts in ((0,), (1,), (2, 3)):
+            first_stage(1, ts, words, [xt_s, xo_s[:, HALF:J]])
 
         wb_raw = sb([P, 2 * N], U8, "wb_raw", "x_scales0")
-        wb_plane = sb([P, N], U8, "wb_plane", "x_scales1")
+        wb_plane = sb([P, N], U8, "wb_plane", "g_xo_scales")
         nc.vector.memset(wb_plane[:].bitcast(I32), 0)
         load_words(wb_raw[:], wb_words[0])
-        wb_rows = wb_scales[0].bitcast(I32).rearrange("(q r) c -> r q c", r=4)
-        for r in range(4):
-            nc.sync.dma_start(out=wb_plane[:].bitcast(I32)[r:P:32, :], in_=wb_rows[r])
+        load_plane(wb_plane, wb_scales)
 
-        board_b = [sb([P, C], F32, f"board_b{t}", tag) for t, tag in enumerate(("x_words0", "x_words1", "w_raw", "ws_plane"))]
+        board_b = [sb([P, C], F32, f"board_b{t}", tag) for t, tag in enumerate(("x_words0", "x_words1", "g_words0", "g_words1"))]
         for t in range(PACK):
             h1 = sb([P, J], F32, f"h1_{t}")
             nc.vector.tensor_copy(out=h1[:], in_=board_a[t][:].indirect(lists[3][:]))
@@ -129,15 +138,17 @@ def tile_list_tworoutes_kernel(tc, xt_words, xt_scales, xo_words, xo_scales, w_w
 
         last = PACK - 1
         hid = sb([P, J, PACK], BF16, "hid")
-        picked = sb([P, last, J], F32, "picked")
+        picked = [sb([P, 2, J], F32, f"picked{u}") for u in range(2)]
         for t in range(last):
-            nc.vector.tensor_copy(out=picked[:, t, :], in_=board_b[t][:].indirect(lists[5][:]))
-        nc.vector.tensor_scalar(out=hid[:, :, 0:last], in0=picked[:].rearrange("p t o -> p o t"), scalar1=0.0, scalar2=None, op0=MAX)
-        tail = [sb([P, HALF], F32, f"tail{h}") for h in range(2)]
-        nc.vector.tensor_copy(out=tail[0][:], in_=board_b[last][:].indirect(lists[5][:, 0:HCOLS]))
-        nc.scalar.activation(tail[1][:], board_b[last][:].indirect(lists[5][:, HCOLS : 2 * HCOLS]), COPY)
+            nc.vector.tensor_copy(out=picked[t // 2][:, t % 2, :], in_=board_b[t][:].indirect(lists[5][:]))
+            if t == 1:
+                nc.vector.tensor_scalar(out=hid[:, :, 0:2], in0=picked[0][:].rearrange("p t o -> p o t"), scalar1=0.0, scalar2=None, op0=MAX)
+        nc.vector.tensor_copy(out=picked[1][:, 1, 0:HALF], in_=board_b[last][:].indirect(lists[5][:, 0:HCOLS]))
+        nc.scalar.activation(picked[1][:, 1, HALF:J], board_b[last][:].indirect(lists[5][:, HCOLS : 2 * HCOLS]), COPY)
         for h in range(2):
-            nc.vector.tensor_scalar(out=hid[:, HALF * h : HALF * (h + 1), last], in0=tail[h][:], scalar1=0.0, scalar2=None, op0=MAX)
+            cols = slice(HALF * h, HALF * (h + 1))
+            nc.vector.tensor_scalar(out=hid[:, cols, 2:PACK], in0=picked[1][:, :, cols].rearrange("p t o -> p o t"),
+                                    scalar1=0.0, scalar2=None, op0=MAX)
 
         out_v = out.rearrange("(m p) (h o) -> h p m o", p=P, h=2)
         for h in range(2):

from contextlib import ExitStack

import concourse.mybir as mybir

F32 = mybir.dt.float32
BF16 = mybir.dt.bfloat16
I32 = mybir.dt.int32
U32 = mybir.dt.uint32
U16 = mybir.dt.uint16
U8 = mybir.dt.uint8
E4M3 = mybir.dt.float8_e4m3fn_x4
E5M2 = mybir.dt.float8_e5m2_x4
E2M1 = mybir.dt.float4_e2m1fn_x4
COPY = mybir.ActivationFunctionType.Copy
MAX = mybir.AluOpType.max

P = 128
PACK = 4
T, J, R, C, N = 1024, 256, 512, 512, 256
HALF = 128
HCOLS = HALF // 16
FLOPS = 2 * (2 * 512 * R * J + R * N * J)


def tile_list_tworoutes_kernel(tc, xt_words, xt_scales, xo_words, xo_scales, w_words, w_scales, w0_words, w0_scales,
                                    wb_words, wb_scales, offs, offs2, offs3, offs4, offs5, offs6, out):
    nc = tc.nc
    with ExitStack() as ctx:
        pool = ctx.enter_context(tc.tile_pool(name="keep", bufs=1))
        psum = ctx.enter_context(tc.psum_pool(name="psum", bufs=1))

        def sb(shape, dtype, name, tag=None):
            return pool.tile(shape, dtype, name=name, tag=tag or name, align_bytes=64)

        lists = [sb([P, J // 16], U16, f"list{i}") for i in range(6)]
        x_words = [sb([P, T], U32, f"x_words{i}") for i in range(2)]
        x_scales = [sb([P, T], U8, f"x_scales{i}") for i in range(2)]
        xs_stage = sb([4, 4, T], U8, "xs_stage")
        ws_stage = sb([4, 4, 2, R], U8, "ws_stage")
        w_raw = sb([P, 2, 2 * R], U8, "w_raw")
        ws_plane = sb([P, 2, R], U8, "ws_plane")
        board_a = [sb([P, C], F32, f"board_a{t}") for t in range(PACK)]

        xs32 = xs_stage[:].rearrange("p q c -> p (q c)").bitcast(I32).rearrange("p (q c) -> p q c", q=4)
        ws32 = ws_stage[:].rearrange("p q i c -> p (q i c)").bitcast(I32).rearrange("p (q i c) -> p q i c", q=4, i=2)
        wsp32 = ws_plane[:].rearrange("p i c -> p (i c)").bitcast(I32).rearrange("p (i c) -> p i c", i=2)
        for t in range(2):
            nc.vector.memset(board_a[t][:], 0.0)
        nc.vector.memset(x_scales[1][:].bitcast(I32), 0)
        for t in range(2, PACK):
            nc.vector.memset(board_a[t][:], 0.0)
        nc.vector.memset(x_scales[0][:].bitcast(I32), 0)
        nc.vector.memset(wsp32, 0)

        def load_words(dst, src):
            nc.sync.dma_start(out=dst.bitcast(I32), in_=src.bitcast(I32))

        def load_rows(dst, src):
            nc.scalar.dma_start(out=dst, in_=src[0].bitcast(I32).rearrange("(q r) c -> r q c", r=4))

        def load_plane(dst, src):
            rows = src[0].bitcast(I32).rearrange("(q r) c -> r q c", r=4)
            for r in range(4):
                nc.sync.dma_start(out=dst[:].bitcast(I32)[r:P:32, :], in_=rows[r])

        load_words(w_raw[:, 0, :], w_words[0])
        load_rows(xs32, xt_scales)
        load_words(w_raw[:, 1, :], w0_words[0])
        load_rows(ws32[:, :, 0, :], w_scales)
        nc.sync.dma_start(lists[0][:], offs)
        load_rows(ws32[:, :, 1, :], w0_scales)
        nc.sync.dma_start(lists[1][:], offs2)
        load_words(x_words[0][:], xt_words[0].rearrange("p c r -> p (c r)"))
        nc.sync.dma_start(lists[2][:], offs3)
        load_words(x_words[1][:], xo_words[0].rearrange("p c r -> p (c r)"))
        for i, src in ((3, offs4), (4, offs5), (5, offs6)):
            nc.sync.dma_start(lists[i][:], src)
        load_plane(x_scales[1], xo_scales)

        for q in range(4):
            nc.vector.tensor_copy(out=x_scales[0][:].bitcast(I32)[32 * q : 32 * q + 4], in_=xs32[:, q, :])
            nc.vector.tensor_copy(out=wsp32[32 * q : 32 * q + 4], in_=ws32[:, q])

        w16 = w_raw[:].rearrange("p i c -> p (i c)").bitcast(U16).rearrange("p (i m t) -> p t i m", i=2, t=PACK)
        ws8 = ws_plane[:].rearrange("p i (m t) -> p t i m", t=PACK)
        w_dealt = sb([P, PACK, 2, 2 * P], U8, "w_dealt")
        wd16 = w_dealt[:].rearrange("p t i c -> p (t i c)").bitcast(U16).rearrange("p (t i m) -> p t i m", t=PACK, i=2)

        def gather(table, i, h, dtype, name):
            got = sb([P, HALF], dtype, f"{name}_{h}", name)
            nc.vector.tensor_copy(out=got[:], in_=table[:].indirect(lists[i][:, HCOLS * h : HCOLS * (h + 1)]))
            return got[:]

        def first_stage(h, ts, words, scales):
            acc = psum.tile([P, len(ts), HALF], F32, name=f"acc{h}_{ts[0]}")
            for u, t in enumerate(ts):
                for i, fmt in enumerate((E5M2, E4M3)):
                    nc.tensor.matmul_mx(out=acc[:, u, :], lhsT=w_dealt[:, t, i, :].bitcast(E2M1), lhsT_scale=ws_dealt[t][:, i, :],
                                        rhs=words[i].bitcast(fmt), rhs_scale=scales[i], start=(i == 0), stop=(i == 1))
            a_sb = sb([P, len(ts), HALF], F32, f"a{h}_{ts[0]}")
            if (h, ts[0]) == (0, 0):
                nc.scalar.activation(a_sb[:], acc[:], COPY)
            else:
                nc.vector.tensor_copy(out=a_sb[:], in_=acc[:])
            for u, t in enumerate(ts):
                nc.scalar.activation(board_a[t][:].indirect(lists[2][:, HCOLS * h : HCOLS * (h + 1)]), a_sb[:, u, :], COPY)

        nc.scalar.copy(out=wd16, in_=w16)
        ws_first = sb([P, 2, P], U8, "ws_first")
        nc.vector.tensor_copy(out=ws_first[:], in_=ws8[:, 0])
        xt_s = gather(x_scales[0], 0, 0, U8, "g_xt_scales")
        words = [gather(x_words[i], i, 0, U32, f"g_words{i}") for i in range(2)]
        xo_s = sb([P, J], U8, "g_xo_scales")
        nc.vector.tensor_copy(out=xo_s[:], in_=x_scales[1][:].indirect(lists[1][:]))
        ws_rest = sb([P, PACK - 1, 2, P], U8, "ws_rest", "x_scales1")
        nc.vector.tensor_copy(out=ws_rest[:, 0:1], in_=ws8[:, 1:2])
        nc.vector.tensor_copy(out=ws_rest[:, 1:3], in_=ws8[:, 2:PACK])
        ws_dealt = [ws_first[:]] + [ws_rest[:, u] for u in range(PACK - 1)]
        for ts in ((0,), (1,), (2, 3)):
            first_stage(0, ts, words, [xt_s, xo_s[:, 0:HALF]])
        xt_s = gather(x_scales[0], 0, 1, U8, "g_xt_scales")
        words = [gather(x_words[i], i, 1, U32, f"g_words{i}") for i in range(2)]
        for ts in ((0,), (1,), (2, 3)):
            first_stage(1, ts, words, [xt_s, xo_s[:, HALF:J]])

        wb_raw = sb([P, 2 * N], U8, "wb_raw", "x_scales0")
        wb_plane = sb([P, N], U8, "wb_plane", "g_xo_scales")
        nc.vector.memset(wb_plane[:].bitcast(I32), 0)
        load_words(wb_raw[:], wb_words[0])
        load_plane(wb_plane, wb_scales)

        board_b = [sb([P, C], F32, f"board_b{t}", tag) for t, tag in enumerate(("x_words0", "x_words1", "g_words0", "g_words1"))]
        for t in range(PACK):
            h1 = sb([P, J], F32, f"h1_{t}")
            nc.vector.tensor_copy(out=h1[:], in_=board_a[t][:].indirect(lists[3][:]))
            nc.vector.memset(board_b[t][:], 0.0)
            nc.scalar.activation(board_b[t][:].indirect(lists[4][:]), h1[:], COPY)

        last = PACK - 1
        hid = sb([P, J, PACK], BF16, "hid")
        picked = [sb([P, 2, J], F32, f"picked{u}") for u in range(2)]
        for t in range(last):
            nc.vector.tensor_copy(out=picked[t // 2][:, t % 2, :], in_=board_b[t][:].indirect(lists[5][:]))
            if t == 1:
                nc.vector.tensor_scalar(out=hid[:, :, 0:2], in0=picked[0][:].rearrange("p t o -> p o t"), scalar1=0.0, scalar2=None, op0=MAX)
        nc.vector.tensor_copy(out=picked[1][:, 1, 0:HALF], in_=board_b[last][:].indirect(lists[5][:, 0:HCOLS]))
        nc.scalar.activation(picked[1][:, 1, HALF:J], board_b[last][:].indirect(lists[5][:, HCOLS : 2 * HCOLS]), COPY)
        for h in range(2):
            cols = slice(HALF * h, HALF * (h + 1))
            nc.vector.tensor_scalar(out=hid[:, cols, 2:PACK], in0=picked[1][:, :, cols].rearrange("p t o -> p o t"),
                                    scalar1=0.0, scalar2=None, op0=MAX)

        out_v = out.rearrange("(m p) (h o) -> h p m o", p=P, h=2)
        for h in range(2):
            codes = sb([P, HALF], U32, f"codes{h}")
            plane = sb([P, HALF], U8, f"plane{h}")
            nc.vector.quantize_mx(out=codes[:].bitcast(E4M3), scales=plane[:],
                                  in_=hid[:, HALF * h : HALF * (h + 1), :].rearrange("p o t -> p (o t)"))
            res = psum.tile([P, 2, HALF], F32, name=f"res{h}")
            for m in range(2):
                nc.tensor.matmul_mx(out=res[:, m, :], lhsT=wb_raw[:, 2 * P * m : 2 * P * (m + 1)].bitcast(E2M1),
                                    lhsT_scale=wb_plane[:, P * m : P * (m + 1)], rhs=codes[:].bitcast(E4M3),
                                    rhs_scale=plane[:], start=True, stop=True)
            res_sb = sb([P, 2, HALF], F32, f"res_sb{h}")
            if h == 0:
                nc.scalar.copy(out=res_sb[:], in_=res[:])
                nc.scalar.dma_start(out=out_v[h], in_=res_sb[:])
            else:
                nc.vector.tensor_copy(out=res_sb[:], in_=res[:])
                nc.sync.dma_start(out=out_v[h], in_=res_sb[:])
